import numpy as np
import ml_dtypes


def mxq(x, axis, fmt="e4m3"):
    dtype, down = {"e4m3": (ml_dtypes.float8_e4m3fn, 7), "e5m2": (ml_dtypes.float8_e5m2, 14)}[fmt]
    v = np.moveaxis(np.asarray(x, np.float32).astype(ml_dtypes.bfloat16).astype(np.float64), axis, -1)
    blocks = v.reshape(v.shape[:-1] + (-1, 32))
    amax = np.abs(blocks).max(-1, keepdims=True)
    byte = np.maximum(np.where(amax > 0, np.frexp(amax)[1] - 1 + 127, 0) - down, 1)
    scale = np.exp2(byte - 127.0)
    codes = (blocks / scale).astype(np.float32).astype(dtype).astype(np.float64)
    return np.moveaxis((codes * scale).reshape(v.shape), -1, axis)


WIDE = False


def mx_kscale(k, group=512):
    if not WIDE:
        return np.ones(k)
    levels = np.array([10, -10, 5, -5, 0])
    if group != 512:
        return np.exp2(np.random.permutation(np.resize(levels, k // group))).repeat(group)
    if k % 512:
        return np.exp2(np.random.permutation(np.resize(levels, k // 32))).repeat(32)
    a = np.empty((k // 512, 16))
    for p in range(k // 512):
        a[p, :8] = np.random.permutation(np.resize(levels, 8))
        for g in range(8):
            far = levels[np.abs(levels - a[p, g]) >= 10]
            a[p, g + 8] = far[np.random.randint(len(far))]
    return np.exp2(a.ravel()).repeat(32)


def f64(x):
    return np.asarray(x).astype(np.float64)


G, D, M, N = 4, 256, 256, 512


def setup_inputs():
    n = np.random.standard_normal
    s = mx_kscale(D, 0)[:, None]
    return {
        "x": (n((G, D, N)) * s).astype(np.float32),
        "w": (n((G, D, M)) / np.sqrt(D) / s).astype(np.float32),
        "r": n((G, M, N)).astype(np.float32),
    }


def reference(x, w, r):
    xq = mxq(f64(x), 1, "e4m3")
    y = mxq(f64(w), 1, "e4m3").transpose(0, 2, 1) @ xq
    y = np.square(np.maximum(y, 0.0))
    y = y + f64(r)
    return y

@@ -1,0 +1,185 @@
+from contextlib import ExitStack
+
+import concourse.mybir as mybir
+
+G, D, M, N = 4, 256, 256, 512
+FLOPS = 2 * G * D * M * N
+
+F32 = mybir.dt.float32
+BF16 = mybir.dt.bfloat16
+U32 = mybir.dt.uint32
+U8 = mybir.dt.uint8
+FP8X4 = mybir.dt.float8_e4m3fn_x4
+ACT = mybir.ActivationFunctionType
+ALU = mybir.AluOpType
+
+P = 128
+PACK = 4
+ROWS = D // PACK
+SIDE = P // ROWS
+PAIRS = G // SIDE
+DEAL = M // P
+RUN = 4
+
+
+def tile_rows_glin_relu2_res_kernel(tc, x, w, r, out):
+    nc = tc.nc
+    with ExitStack() as ctx:
+        sb = ctx.enter_context(tc.tile_pool(name="sb", bufs=1))
+        psum = ctx.enter_context(tc.psum_pool(name="psum", bufs=1))
+
+        def tiles(pool, name, count, shape, dtype, align):
+            return [pool.tile(shape, dtype, name="%s%d" % (name, i), align_bytes=align) for i in range(count)]
+
+        x_raw = tiles(sb, "x_raw", PAIRS, [P, PACK, N], F32, 64)
+        w_raw = tiles(sb, "w_raw", PAIRS, [P, PACK, M], F32, 64)
+        x_bf = tiles(sb, "x_bf", PAIRS, [P, N, PACK], BF16, 64)
+        w_bf = tiles(sb, "w_bf", PAIRS, [P, DEAL, P, PACK], BF16, 64)
+        x_codes = tiles(sb, "x_codes", PAIRS, [P, N], U32, 64)
+        x_scales = tiles(sb, "x_scales", PAIRS, [P, N], U8, 64)
+        w_codes = tiles(sb, "w_codes", PAIRS, [P, M], U32, 64)
+        w_scales = tiles(sb, "w_scales", PAIRS, [P, M], U8, 64)
+        res = tiles(sb, "res", PAIRS, [P, SIDE, DEAL, N], F32, 64)
+        relu = tiles(sb, "relu", G, [P, DEAL, N], F32, 64)
+        sq = tiles(sb, "sq", G, [P, DEAL, N], F32, 64)
+        result = tiles(sb, "result", G, [P, DEAL, N], F32, 64)
+        z = [[psum.tile([P, N], F32, name="z%d_%d" % (g, t)) for t in range(DEAL)] for g in range(G)]
+        warm = sb.tile([P, 2], F32)
+
+        def load_x(q):
+            src = x[SIDE * q : SIDE * (q + 1)].rearrange("c (p j) n -> (c p) j n", j=PACK)
+            nc.sync.dma_start(out=x_raw[q][:], in_=src)
+
+        def load_w(q):
+            src = w[SIDE * q : SIDE * (q + 1)].rearrange("c (p j) m -> (c p) j m", j=PACK)
+            nc.sync.dma_start(out=w_raw[q][:], in_=src)
+
+        def load_r(g0, g1):
+            src = r[g0:g1].rearrange("c (p t) n -> p c t n", t=DEAL)
+            q, c = divmod(g0, SIDE)
+            nc.sync.dma_start(out=res[q][:, c : c + g1 - g0], in_=src)
+
+        def copy(engine, dst, src):
+            if engine == "V":
+                nc.vector.tensor_copy(out=dst, in_=src)
+            else:
+                nc.scalar.copy(out=dst, in_=src)
+
+        def copy_x(engine, q, n0, n1):
+            dst = x_bf[q][:, n0:n1, :].rearrange("p (c i) j -> p c j i", i=RUN)
+            src = x_raw[q][:, :, n0:n1].rearrange("p j (c i) -> p c j i", i=RUN)
+            copy(engine, dst, src)
+
+        def copy_w(engine, q, s0, s1):
+            dst = w_bf[q][:, :, s0:s1, :].rearrange("p t (c i) j -> p c j i t", i=RUN // DEAL)
+            src = w_raw[q][:, :, DEAL * s0 : DEAL * s1].rearrange("p j (c i t) -> p c j i t", i=RUN // DEAL, t=DEAL)
+            copy(engine, dst, src)
+
+        def quant_x(q, n0, n1):
+            nc.vector.quantize_mx(
+                out=x_codes[q][:, n0:n1].bitcast(FP8X4),
+                scales=x_scales[q][:, n0:n1],
+                in_=x_bf[q][:, n0:n1, :].rearrange("p n j -> p (n j)"),
+            )
+
+        def quant_w(q):
+            nc.vector.quantize_mx(
+                out=w_codes[q][:].bitcast(FP8X4),
+                scales=w_scales[q][:],
+                in_=w_bf[q][:].rearrange("p t s j -> p (t s j)"),
+            )
+
+        def mm(g, t):
+            q, c = divmod(g, SIDE)
+            rows = slice(ROWS * c, ROWS * (c + 1))
+            cols = slice(P * t, P * (t + 1))
+            nc.tensor.matmul_mx(
+                out=z[g][t][:],
+                lhsT=w_codes[q][rows, cols].bitcast(FP8X4),
+                lhsT_scale=w_scales[q][rows, cols],
+                rhs=x_codes[q][rows, :].bitcast(FP8X4),
+                rhs_scale=x_scales[q][rows, :],
+                start=True,
+                stop=True,
+            )
+
+        def do_relu(engine, g, t):
+            if engine == "V":
+                nc.vector.tensor_scalar(out=relu[g][:, t, :], in0=z[g][t][:], scalar1=0.0, scalar2=None, op0=ALU.max)
+            else:
+                nc.scalar.activation(out=relu[g][:, t, :], in_=z[g][t][:], func=ACT.Relu)
+
+        def do_sq(engine, g, t):
+            if engine == "V":
+                nc.vector.tensor_tensor(out=sq[g][:, t, :], in0=z[g][t][:], in1=relu[g][:, t, :], op=ALU.mult)
+            else:
+                nc.scalar.activation(out=sq[g][:, t, :], in_=relu[g][:, t, :], func=ACT.Square)
+
+        def do_add(engine, g, t):
+            q, c = divmod(g, SIDE)
+            eng = nc.vector if engine == "V" else nc.gpsimd
+            eng.tensor_tensor(out=result[g][:, t, :], in0=sq[g][:, t, :], in1=res[q][:, c, t, :], op=ALU.add)
+
+        def store(g, t0, t1):
+            dst = out[g].rearrange("(p t) n -> p t n", t=DEAL)
+            nc.sync.dma_start(out=dst[:, t0:t1, :], in_=result[g][:, t0:t1, :])
+
+        with tc.manual_schedule():
+            load_x(0)
+            load_w(0)
+            load_x(1)
+            load_w(1)
+            load_r(0, 1)
+            load_r(1, 2)
+            load_r(2, 4)
+            nc.gpsimd.memset(warm[:, 0:1], 0.0)
+            nc.scalar.activation(out=warm[:, 1:2], in_=warm[:, 0:1], func=ACT.Square)
+            copy_x("V", 0, 0, 256)
+            copy_x("S", 0, 320, 512)
+            copy_x("V", 0, 256, 320)
+            quant_x(0, 0, 256)
+            quant_x(0, 256, 512)
+            copy_w("S", 0, 80, 128)
+            copy_w("V", 0, 0, 80)
+            quant_w(0)
+            mm(0, 0)
+            mm(1, 0)
+            mm(0, 1)
+            mm(1, 1)
+            do_relu("S", 0, 0)
+            do_relu("V", 1, 0)
+            do_relu("S", 0, 1)
+            copy_x("V", 1, 0, 512)
+            do_sq("S", 0, 0)
+            do_relu("S", 1, 1)
+            copy_w("V", 1, 0, 128)
+            quant_x(1, 0, 512)
+            quant_w(1)
+            mm(2, 0)
+            mm(3, 0)
+            mm(2, 1)
+            mm(3, 1)
+            do_sq("S", 0, 1)
+            do_sq("S", 1, 0)
+            do_sq("S", 1, 1)
+            do_add("V", 0, 0)
+            do_add("V", 0, 1)
+            store(0, 0, 2)
+            do_relu("S", 2, 0)
+            do_relu("S", 2, 1)
+            do_sq("S", 2, 0)
+            do_add("V", 1, 0)
+            do_add("V", 1, 1)
+            store(1, 0, 2)
+            do_sq("S", 2, 1)
+            do_relu("V", 3, 0)
+            do_relu("S", 3, 1)
+            do_add("V", 2, 0)
+            do_sq("S", 3, 0)
+            do_add("V", 2, 1)
+            store(2, 0, 2)
+            do_sq("S", 3, 1)
+            do_add("V", 3, 0)
+            store(3, 0, 1)
+            do_add("V", 3, 1)
+            store(3, 1, 2)

@@ -20,6 +20,9 @@ SIDE = P // ROWS
 PAIRS = G // SIDE
 DEAL = M // P
 RUN = 4
+MODE = "tt"
+NT = 512
+HALF = N // 2
 
 
 def tile_rows_glin_relu2_res_kernel(tc, x, w, r, out):
@@ -46,9 +49,9 @@ def tile_rows_glin_relu2_res_kernel(tc, x, w, r, out):
         z = [[psum.tile([P, N], F32, name="z%d_%d" % (g, t)) for t in range(DEAL)] for g in range(G)]
         warm = sb.tile([P, 2], F32)
 
-        def load_x(q):
+        def load_x(q, n0, n1):
             src = x[SIDE * q : SIDE * (q + 1)].rearrange("c (p j) n -> (c p) j n", j=PACK)
-            nc.sync.dma_start(out=x_raw[q][:], in_=src)
+            nc.sync.dma_start(out=x_raw[q][:, :, n0:n1], in_=src[:, :, n0:n1])
 
         def load_w(q):
             src = w[SIDE * q : SIDE * (q + 1)].rearrange("c (p j) m -> (c p) j m", j=PACK)
@@ -75,6 +78,11 @@ def tile_rows_glin_relu2_res_kernel(tc, x, w, r, out):
             src = w_raw[q][:, :, DEAL * s0 : DEAL * s1].rearrange("p j (c i t) -> p c j i t", i=RUN // DEAL, t=DEAL)
             copy(engine, dst, src)
 
+        def copy_wt(engine, q, t):
+            dst = w_bf[q][:, t, :, :].rearrange("p (c i) j -> p c j i", i=RUN // DEAL)
+            src = w_raw[q][:].rearrange("p j (c i t) -> p t c j i", i=RUN // DEAL, t=DEAL)[:, t]
+            copy(engine, dst, src)
+
         def quant_x(q, n0, n1):
             nc.vector.quantize_mx(
                 out=x_codes[q][:, n0:n1].bitcast(FP8X4),
@@ -82,104 +90,123 @@ def tile_rows_glin_relu2_res_kernel(tc, x, w, r, out):
                 in_=x_bf[q][:, n0:n1, :].rearrange("p n j -> p (n j)"),
             )
 
-        def quant_w(q):
+        def quant_w(q, t0, t1):
             nc.vector.quantize_mx(
-                out=w_codes[q][:].bitcast(FP8X4),
-                scales=w_scales[q][:],
-                in_=w_bf[q][:].rearrange("p t s j -> p (t s j)"),
+                out=w_codes[q][:, P * t0 : P * t1].bitcast(FP8X4),
+                scales=w_scales[q][:, P * t0 : P * t1],
+                in_=w_bf[q][:, t0:t1].rearrange("p t s j -> p (t s j)"),
             )
 
-        def mm(g, t):
+        def zview(g, t0, t1, n0, n1):
+            if MODE[g // SIDE] == "t":
+                return z[g][t0][:, n0:n1].unsqueeze(1)
+            h, o = divmod(n0, HALF)
+            return z[g][h][:].rearrange("p (t n) -> p t n", t=DEAL)[:, t0:t1, o : o + n1 - n0]
+
+        def mm(g, t0, t1, n0, n1):
             q, c = divmod(g, SIDE)
             rows = slice(ROWS * c, ROWS * (c + 1))
-            cols = slice(P * t, P * (t + 1))
-            nc.tensor.matmul_mx(
-                out=z[g][t][:],
-                lhsT=w_codes[q][rows, cols].bitcast(FP8X4),
-                lhsT_scale=w_scales[q][rows, cols],
-                rhs=x_codes[q][rows, :].bitcast(FP8X4),
-                rhs_scale=x_scales[q][rows, :],
-                start=True,
-                stop=True,
-            )
+            for t in range(t0, t1):
+                cols = slice(P * t, P * (t + 1))
+                for n in range(n0, n1, NT):
+                    nc.tensor.matmul_mx(
+                        out=zview(g, t, t + 1, n, n + NT)[:, 0, :],
+                        lhsT=w_codes[q][rows, cols].bitcast(FP8X4),
+                        lhsT_scale=w_scales[q][rows, cols],
+                        rhs=x_codes[q][rows, n : n + NT].bitcast(FP8X4),
+                        rhs_scale=x_scales[q][rows, n : n + NT],
+                        start=True,
+                        stop=True,
+                    )
 
-        def do_relu(engine, g, t):
+        def do_relu(engine, g, t0, t1, n0, n1):
+            dst = relu[g][:, t0:t1, n0:n1]
             if engine == "V":
-                nc.vector.tensor_scalar(out=relu[g][:, t, :], in0=z[g][t][:], scalar1=0.0, scalar2=None, op0=ALU.max)
+                nc.vector.tensor_scalar(out=dst, in0=zview(g, t0, t1, n0, n1), scalar1=0.0, scalar2=None, op0=ALU.max)
             else:
-                nc.scalar.activation(out=relu[g][:, t, :], in_=z[g][t][:], func=ACT.Relu)
+                nc.scalar.activation(out=dst, in_=zview(g, t0, t1, n0, n1), func=ACT.Relu)
 
-        def do_sq(engine, g, t):
+        def do_sq(engine, g, t0, t1, n0, n1):
+            dst = sq[g][:, t0:t1, n0:n1]
+            src = relu[g][:, t0:t1, n0:n1]
             if engine == "V":
-                nc.vector.tensor_tensor(out=sq[g][:, t, :], in0=z[g][t][:], in1=relu[g][:, t, :], op=ALU.mult)
+                nc.vector.tensor_tensor(out=dst, in0=src, in1=src, op=ALU.mult)
             else:
-                nc.scalar.activation(out=sq[g][:, t, :], in_=relu[g][:, t, :], func=ACT.Square)
+                nc.scalar.activation(out=dst, in_=src, func=ACT.Square)
 
-        def do_add(engine, g, t):
+        def do_add(engine, g, t0, t1, n0, n1):
             q, c = divmod(g, SIDE)
             eng = nc.vector if engine == "V" else nc.gpsimd
-            eng.tensor_tensor(out=result[g][:, t, :], in0=sq[g][:, t, :], in1=res[q][:, c, t, :], op=ALU.add)
+            eng.tensor_tensor(out=result[g][:, t0:t1, n0:n1], in0=sq[g][:, t0:t1, n0:n1], in1=res[q][:, c, t0:t1, n0:n1], op=ALU.add)
 
-        def store(g, t0, t1):
+        def store(g, t0, t1, n0, n1):
             dst = out[g].rearrange("(p t) n -> p t n", t=DEAL)
-            nc.sync.dma_start(out=dst[:, t0:t1, :], in_=result[g][:, t0:t1, :])
+            nc.sync.dma_start(out=dst[:, t0:t1, n0:n1], in_=result[g][:, t0:t1, n0:n1])
 
         with tc.manual_schedule():
-            load_x(0)
+            load_x(0, 0, 512)
             load_w(0)
-            load_x(1)
             load_w(1)
+            load_x(1, 0, 512)
             load_r(0, 1)
             load_r(1, 2)
-            load_r(2, 4)
+            load_r(2, 3)
+            load_r(3, 4)
             nc.gpsimd.memset(warm[:, 0:1], 0.0)
             nc.scalar.activation(out=warm[:, 1:2], in_=warm[:, 0:1], func=ACT.Square)
             copy_x("V", 0, 0, 256)
             copy_x("S", 0, 320, 512)
             copy_x("V", 0, 256, 320)
             quant_x(0, 0, 256)
+            copy_wt("S", 0, 1)
+            copy_wt("V", 0, 0)
             quant_x(0, 256, 512)
-            copy_w("S", 0, 80, 128)
-            copy_w("V", 0, 0, 80)
-            quant_w(0)
-            mm(0, 0)
-            mm(1, 0)
-            mm(0, 1)
-            mm(1, 1)
-            do_relu("S", 0, 0)
-            do_relu("V", 1, 0)
-            do_relu("S", 0, 1)
-            copy_x("V", 1, 0, 512)
-            do_sq("S", 0, 0)
-            do_relu("S", 1, 1)
-            copy_w("V", 1, 0, 128)
-            quant_x(1, 0, 512)
-            quant_w(1)
-            mm(2, 0)
-            mm(3, 0)
-            mm(2, 1)
-            mm(3, 1)
-            do_sq("S", 0, 1)
-            do_sq("S", 1, 0)
-            do_sq("S", 1, 1)
-            do_add("V", 0, 0)
-            do_add("V", 0, 1)
-            store(0, 0, 2)
-            do_relu("S", 2, 0)
-            do_relu("S", 2, 1)
-            do_sq("S", 2, 0)
-            do_add("V", 1, 0)
-            do_add("V", 1, 1)
-            store(1, 0, 2)
-            do_sq("S", 2, 1)
-            do_relu("V", 3, 0)
-            do_relu("S", 3, 1)
-            do_add("V", 2, 0)
-            do_sq("S", 3, 0)
-            do_add("V", 2, 1)
-            store(2, 0, 2)
-            do_sq("S", 3, 1)
-            do_add("V", 3, 0)
-            store(3, 0, 1)
-            do_add("V", 3, 1)
-            store(3, 1, 2)
+            quant_w(0, 0, 1)
+            quant_w(0, 1, 2)
+            mm(0, 0, 1, 0, 512)
+            mm(1, 0, 1, 0, 512)
+            mm(0, 1, 2, 0, 512)
+            mm(1, 1, 2, 0, 512)
+            copy_w("V", 1, 0, 80)
+            copy_w("S", 1, 80, 128)
+            quant_w(1, 0, 2)
+            do_relu("S", 0, 0, 1, 0, 512)
+            do_relu("V", 1, 0, 1, 0, 512)
+            do_relu("S", 0, 1, 2, 0, 512)
+            do_relu("V", 1, 1, 2, 0, 512)
+            do_sq("S", 0, 0, 1, 0, 512)
+            copy_x("V", 1, 0, 256)
+            copy_x("S", 1, 384, 512)
+            copy_x("V", 1, 256, 384)
+            quant_x(1, 0, 256)
+            quant_x(1, 256, 512)
+            mm(2, 0, 1, 0, 512)
+            mm(3, 0, 1, 0, 512)
+            mm(2, 1, 2, 0, 512)
+            mm(3, 1, 2, 0, 512)
+            do_sq("S", 0, 1, 2, 0, 512)
+            do_sq("S", 1, 0, 1, 0, 512)
+            do_sq("S", 1, 1, 2, 0, 512)
+            do_add("V", 0, 0, 1, 0, 512)
+            do_add("V", 0, 1, 2, 0, 512)
+            store(0, 0, 2, 0, 512)
+            do_add("V", 1, 0, 1, 0, 512)
+            do_add("V", 1, 1, 2, 0, 512)
+            store(1, 0, 2, 0, 512)
+            do_relu("S", 2, 0, 1, 0, 512)
+            do_relu("S", 3, 0, 1, 0, 512)
+            do_sq("S", 2, 0, 1, 0, 512)
+            do_sq("S", 3, 0, 1, 0, 512)
+            do_relu("V", 2, 1, 2, 0, 512)
+            do_relu("V", 3, 1, 2, 0, 256)
+            do_relu("S", 3, 1, 2, 256, 512)
+            do_sq("S", 2, 1, 2, 0, 512)
+            do_sq("S", 3, 1, 2, 0, 512)
+            do_add("V", 2, 0, 1, 0, 512)
+            store(2, 0, 1, 0, 512)
+            do_add("V", 3, 0, 1, 0, 512)
+            store(3, 0, 1, 0, 512)
+            do_add("V", 2, 1, 2, 0, 512)
+            store(2, 1, 2, 0, 512)
+            do_add("V", 3, 1, 2, 0, 512)
+            store(3, 1, 2, 0, 512)

@@ -46,7 +46,25 @@ def tile_rows_glin_relu2_res_kernel(tc, x, w, r, out):
         relu = tiles(sb, "relu", G, [P, DEAL, N], F32, 64)
         sq = tiles(sb, "sq", G, [P, DEAL, N], F32, 64)
         result = tiles(sb, "result", G, [P, DEAL, N], F32, 64)
-        z = [[psum.tile([P, N], F32, name="z%d_%d" % (g, t)) for t in range(DEAL)] for g in range(G)]
+        banks = [psum.tile([P, N], F32, name="bank%d" % i) for i in range(8)]
+        z = [[banks[0], banks[1]], [banks[2], banks[3]], [banks[4], banks[0]], [banks[5], banks[6]]]
+        idle_bank = banks[7]
+        idle_bf = sb.tile([P, N * PACK], BF16, align_bytes=64)
+        idle_codes = sb.tile([P, N], U32, align_bytes=64)
+        idle_scales = sb.tile([P, N], U8, align_bytes=64)
+
+        def idle_passes(count, codes, scales):
+            for i in range(count):
+                nc.tensor.matmul_mx(
+                    out=idle_bank[:],
+                    lhsT=codes[:, 0:P].bitcast(FP8X4),
+                    lhsT_scale=scales[:, 0:P],
+                    rhs=idle_codes[:].bitcast(FP8X4),
+                    rhs_scale=idle_scales[:],
+                    start=True,
+                    stop=True,
+                )
+
         warm = sb.tile([P, 2], F32)
 
         def load_x(q, n0, n1):
@@ -78,9 +96,9 @@ def tile_rows_glin_relu2_res_kernel(tc, x, w, r, out):
             src = w_raw[q][:, :, DEAL * s0 : DEAL * s1].rearrange("p j (c i t) -> p c j i t", i=RUN // DEAL, t=DEAL)
             copy(engine, dst, src)
 
-        def copy_wt(engine, q, t):
-            dst = w_bf[q][:, t, :, :].rearrange("p (c i) j -> p c j i", i=RUN // DEAL)
-            src = w_raw[q][:].rearrange("p j (c i t) -> p t c j i", i=RUN // DEAL, t=DEAL)[:, t]
+        def copy_wt(engine, q, t, s0, s1):
+            dst = w_bf[q][:, t, s0:s1, :].rearrange("p (c i) j -> p c j i", i=RUN // DEAL)
+            src = w_raw[q][:, :, DEAL * s0 : DEAL * s1].rearrange("p j (c i t) -> p t c j i", i=RUN // DEAL, t=DEAL)[:, t]
             copy(engine, dst, src)
 
         def quant_x(q, n0, n1):
@@ -154,12 +172,16 @@ def tile_rows_glin_relu2_res_kernel(tc, x, w, r, out):
             load_r(3, 4)
             nc.gpsimd.memset(warm[:, 0:1], 0.0)
             nc.scalar.activation(out=warm[:, 1:2], in_=warm[:, 0:1], func=ACT.Square)
+            nc.vector.memset(idle_bf[:].bitcast(mybir.dt.int32), 0)
+            nc.vector.quantize_mx(out=idle_codes[:].bitcast(FP8X4), scales=idle_scales[:], in_=idle_bf[:])
+            idle_passes(8, idle_codes, idle_scales)
             copy_x("V", 0, 0, 256)
             copy_x("S", 0, 320, 512)
             copy_x("V", 0, 256, 320)
             quant_x(0, 0, 256)
-            copy_wt("S", 0, 1)
-            copy_wt("V", 0, 0)
+            idle_passes(2, x_codes[0], x_scales[0])
+            copy_wt("S", 0, 1, 0, 128)
+            copy_wt("V", 0, 0, 0, 128)
             quant_x(0, 256, 512)
             quant_w(0, 0, 1)
             quant_w(0, 1, 2)
@@ -170,6 +192,7 @@ def tile_rows_glin_relu2_res_kernel(tc, x, w, r, out):
             copy_w("V", 1, 0, 80)
             copy_w("S", 1, 80, 128)
             quant_w(1, 0, 2)
+            idle_passes(8, w_codes[1], w_scales[1])
             do_relu("S", 0, 0, 1, 0, 512)
             do_relu("V", 1, 0, 1, 0, 512)
             do_relu("S", 0, 1, 2, 0, 512)
@@ -179,6 +202,7 @@ def tile_rows_glin_relu2_res_kernel(tc, x, w, r, out):
             copy_x("S", 1, 384, 512)
             copy_x("V", 1, 256, 384)
             quant_x(1, 0, 256)
+            idle_passes(1, x_codes[1], x_scales[1])
             quant_x(1, 256, 512)
             mm(2, 0, 1, 0, 512)
             mm(3, 0, 1, 0, 512)

@@ -20,8 +20,6 @@ SIDE = P // ROWS
 PAIRS = G // SIDE
 DEAL = M // P
 RUN = 4
-MODE = "tt"
-NT = 512
 HALF = N // 2
 
 
@@ -31,45 +29,26 @@ def tile_rows_glin_relu2_res_kernel(tc, x, w, r, out):
         sb = ctx.enter_context(tc.tile_pool(name="sb", bufs=1))
         psum = ctx.enter_context(tc.psum_pool(name="psum", bufs=1))
 
-        def tiles(pool, name, count, shape, dtype, align):
-            return [pool.tile(shape, dtype, name="%s%d" % (name, i), align_bytes=align) for i in range(count)]
+        def tiles(name, count, shape, dtype):
+            return [sb.tile(shape, dtype, name="%s%d" % (name, i), align_bytes=64) for i in range(count)]
 
-        x_raw = tiles(sb, "x_raw", PAIRS, [P, PACK, N], F32, 64)
-        w_raw = tiles(sb, "w_raw", PAIRS, [P, PACK, M], F32, 64)
-        x_bf = tiles(sb, "x_bf", PAIRS, [P, N, PACK], BF16, 64)
-        w_bf = tiles(sb, "w_bf", PAIRS, [P, DEAL, P, PACK], BF16, 64)
-        x_codes = tiles(sb, "x_codes", PAIRS, [P, N], U32, 64)
-        x_scales = tiles(sb, "x_scales", PAIRS, [P, N], U8, 64)
-        w_codes = tiles(sb, "w_codes", PAIRS, [P, M], U32, 64)
-        w_scales = tiles(sb, "w_scales", PAIRS, [P, M], U8, 64)
-        res = tiles(sb, "res", PAIRS, [P, SIDE, DEAL, N], F32, 64)
-        relu = tiles(sb, "relu", G, [P, DEAL, N], F32, 64)
-        sq = tiles(sb, "sq", G, [P, DEAL, N], F32, 64)
-        result = tiles(sb, "result", G, [P, DEAL, N], F32, 64)
-        banks = [psum.tile([P, N], F32, name="bank%d" % i) for i in range(8)]
-        z = [[banks[0], banks[1]], [banks[2], banks[3]], [banks[4], banks[0]], [banks[5], banks[6]]]
-        idle_bank = banks[7]
-        idle_bf = sb.tile([P, N * PACK], BF16, align_bytes=64)
-        idle_codes = sb.tile([P, N], U32, align_bytes=64)
-        idle_scales = sb.tile([P, N], U8, align_bytes=64)
+        x_raw = tiles("x_raw", PAIRS, [P, PACK, N], F32)
+        w_raw = tiles("w_raw", PAIRS, [P, PACK, M], F32)
+        x_bf = tiles("x_bf", PAIRS, [P, N, PACK], BF16)
+        w_bf = tiles("w_bf", PAIRS, [P, DEAL, P, PACK], BF16)
+        x_codes = tiles("x_codes", PAIRS, [P, N], U32)
+        x_scales = tiles("x_scales", PAIRS, [P, N], U8)
+        w_codes = tiles("w_codes", PAIRS, [P, M], U32)
+        w_scales = tiles("w_scales", PAIRS, [P, M], U8)
+        res = tiles("res", PAIRS, [P, SIDE, DEAL, N], F32)
+        relu = tiles("relu", G, [P, DEAL, N], F32)
+        sq = tiles("sq", G, [P, DEAL, N], F32)
+        result = tiles("result", G, [P, DEAL, N], F32)
+        z = [[psum.tile([P, N], F32, name="z%d%d" % (g, t)) for t in range(DEAL)] for g in range(G)]
 
-        def idle_passes(count, codes, scales):
-            for i in range(count):
-                nc.tensor.matmul_mx(
-                    out=idle_bank[:],
-                    lhsT=codes[:, 0:P].bitcast(FP8X4),
-                    lhsT_scale=scales[:, 0:P],
-                    rhs=idle_codes[:].bitcast(FP8X4),
-                    rhs_scale=idle_scales[:],
-                    start=True,
-                    stop=True,
-                )
-
-        warm = sb.tile([P, 2], F32)
-
-        def load_x(q, n0, n1):
+        def load_x(q, j0=0, j1=PACK):
             src = x[SIDE * q : SIDE * (q + 1)].rearrange("c (p j) n -> (c p) j n", j=PACK)
-            nc.sync.dma_start(out=x_raw[q][:, :, n0:n1], in_=src[:, :, n0:n1])
+            nc.sync.dma_start(out=x_raw[q][:, j0:j1], in_=src[:, j0:j1])
 
         def load_w(q):
             src = w[SIDE * q : SIDE * (q + 1)].rearrange("c (p j) m -> (c p) j m", j=PACK)
@@ -83,22 +62,23 @@ def tile_rows_glin_relu2_res_kernel(tc, x, w, r, out):
         def copy(engine, dst, src):
             if engine == "V":
                 nc.vector.tensor_copy(out=dst, in_=src)
-            else:
+            elif engine == "S":
                 nc.scalar.copy(out=dst, in_=src)
+            else:
+                nc.gpsimd.tensor_scalar(out=dst, in0=src, scalar1=1.0, scalar2=0.0, op0=ALU.mult, op1=ALU.add)
 
-        def copy_x(engine, q, n0, n1):
-            dst = x_bf[q][:, n0:n1, :].rearrange("p (c i) j -> p c j i", i=RUN)
-            src = x_raw[q][:, :, n0:n1].rearrange("p j (c i) -> p c j i", i=RUN)
+        def copy_x(engine, q, n0, n1, j0=0, j1=PACK):
+            dst = x_bf[q][:, n0:n1, j0:j1].rearrange("p (c i) j -> p c j i", i=RUN)
+            src = x_raw[q][:, j0:j1, n0:n1].rearrange("p j (c i) -> p c j i", i=RUN)
             copy(engine, dst, src)
 
-        def copy_w(engine, q, s0, s1):
-            dst = w_bf[q][:, :, s0:s1, :].rearrange("p t (c i) j -> p c j i t", i=RUN // DEAL)
-            src = w_raw[q][:, :, DEAL * s0 : DEAL * s1].rearrange("p j (c i t) -> p c j i t", i=RUN // DEAL, t=DEAL)
-            copy(engine, dst, src)
-
-        def copy_wt(engine, q, t, s0, s1):
-            dst = w_bf[q][:, t, s0:s1, :].rearrange("p (c i) j -> p c j i", i=RUN // DEAL)
-            src = w_raw[q][:, :, DEAL * s0 : DEAL * s1].rearrange("p j (c i t) -> p t c j i", i=RUN // DEAL, t=DEAL)[:, t]
+        def copy_w(engine, q, t0, t1, s0=0, s1=P):
+            if t1 - t0 == DEAL:
+                dst = w_bf[q][:, :, s0:s1, :].rearrange("p t (c i) j -> p c j i t", i=RUN // DEAL)
+                src = w_raw[q][:, :, DEAL * s0 : DEAL * s1].rearrange("p j (c i t) -> p c j i t", i=RUN // DEAL, t=DEAL)
+            else:
+                dst = w_bf[q][:, t0, s0:s1, :].rearrange("p (c i) j -> p c j i", i=RUN // DEAL)
+                src = w_raw[q][:, :, DEAL * s0 : DEAL * s1].rearrange("p j (c i t) -> p t c j i", i=RUN // DEAL, t=DEAL)[:, t0]
             copy(engine, dst, src)
 
         def quant_x(q, n0, n1):
@@ -115,122 +95,113 @@ def tile_rows_glin_relu2_res_kernel(tc, x, w, r, out):
                 in_=w_bf[q][:, t0:t1].rearrange("p t s j -> p (t s j)"),
             )
 
-        def zview(g, t0, t1, n0, n1):
-            if MODE[g // SIDE] == "t":
-                return z[g][t0][:, n0:n1].unsqueeze(1)
-            h, o = divmod(n0, HALF)
-            return z[g][h][:].rearrange("p (t n) -> p t n", t=DEAL)[:, t0:t1, o : o + n1 - n0]
-
-        def mm(g, t0, t1, n0, n1):
+        def mm(g, t):
             q, c = divmod(g, SIDE)
             rows = slice(ROWS * c, ROWS * (c + 1))
-            for t in range(t0, t1):
-                cols = slice(P * t, P * (t + 1))
-                for n in range(n0, n1, NT):
-                    nc.tensor.matmul_mx(
-                        out=zview(g, t, t + 1, n, n + NT)[:, 0, :],
-                        lhsT=w_codes[q][rows, cols].bitcast(FP8X4),
-                        lhsT_scale=w_scales[q][rows, cols],
-                        rhs=x_codes[q][rows, n : n + NT].bitcast(FP8X4),
-                        rhs_scale=x_scales[q][rows, n : n + NT],
-                        start=True,
-                        stop=True,
-                    )
+            cols = slice(P * t, P * (t + 1))
+            nc.tensor.matmul_mx(
+                out=z[g][t][:],
+                lhsT=w_codes[q][rows, cols].bitcast(FP8X4),
+                lhsT_scale=w_scales[q][rows, cols],
+                rhs=x_codes[q][rows, :].bitcast(FP8X4),
+                rhs_scale=x_scales[q][rows, :],
+                start=True,
+                stop=True,
+            )
 
-        def do_relu(engine, g, t0, t1, n0, n1):
-            dst = relu[g][:, t0:t1, n0:n1]
+        def do_relu(engine, g, t, n0=0, n1=N):
+            dst = relu[g][:, t, n0:n1]
             if engine == "V":
-                nc.vector.tensor_scalar(out=dst, in0=zview(g, t0, t1, n0, n1), scalar1=0.0, scalar2=None, op0=ALU.max)
+                nc.vector.tensor_scalar(out=dst, in0=z[g][t][:, n0:n1], scalar1=0.0, scalar2=None, op0=ALU.max)
             else:
-                nc.scalar.activation(out=dst, in_=zview(g, t0, t1, n0, n1), func=ACT.Relu)
+                nc.scalar.activation(out=dst, in_=z[g][t][:, n0:n1], func=ACT.Relu)
 
-        def do_sq(engine, g, t0, t1, n0, n1):
+        def do_sq(engine, g, t0, t1=None, n0=0, n1=N):
+            t1 = t0 + 1 if t1 is None else t1
             dst = sq[g][:, t0:t1, n0:n1]
             src = relu[g][:, t0:t1, n0:n1]
             if engine == "V":
-                nc.vector.tensor_tensor(out=dst, in0=src, in1=src, op=ALU.mult)
-            else:
+                nc.vector.tensor_tensor(out=dst[:, 0], in0=z[g][t0][:, n0:n1], in1=src[:, 0], op=ALU.mult)
+            elif engine == "S":
                 nc.scalar.activation(out=dst, in_=src, func=ACT.Square)
+            else:
+                nc.gpsimd.tensor_tensor(out=dst, in0=src, in1=src, op=ALU.mult)
 
-        def do_add(engine, g, t0, t1, n0, n1):
+        def do_add(engine, g, t0, t1=None, n0=0, n1=N):
+            t1 = t0 + 1 if t1 is None else t1
             q, c = divmod(g, SIDE)
             eng = nc.vector if engine == "V" else nc.gpsimd
             eng.tensor_tensor(out=result[g][:, t0:t1, n0:n1], in0=sq[g][:, t0:t1, n0:n1], in1=res[q][:, c, t0:t1, n0:n1], op=ALU.add)
 
-        def store(g, t0, t1, n0, n1):
+        def store(g, t0, t1, n0=0, n1=N):
             dst = out[g].rearrange("(p t) n -> p t n", t=DEAL)
             nc.sync.dma_start(out=dst[:, t0:t1, n0:n1], in_=result[g][:, t0:t1, n0:n1])
 
         with tc.manual_schedule():
-            load_x(0, 0, 512)
+            load_x(0)
             load_w(0)
             load_w(1)
-            load_x(1, 0, 512)
+            load_x(1)
             load_r(0, 1)
             load_r(1, 2)
-            load_r(2, 3)
-            load_r(3, 4)
-            nc.gpsimd.memset(warm[:, 0:1], 0.0)
-            nc.scalar.activation(out=warm[:, 1:2], in_=warm[:, 0:1], func=ACT.Square)
-            nc.vector.memset(idle_bf[:].bitcast(mybir.dt.int32), 0)
-            nc.vector.quantize_mx(out=idle_codes[:].bitcast(FP8X4), scales=idle_scales[:], in_=idle_bf[:])
-            idle_passes(8, idle_codes, idle_scales)
+            load_r(2, 4)
             copy_x("V", 0, 0, 256)
             copy_x("S", 0, 320, 512)
             copy_x("V", 0, 256, 320)
             quant_x(0, 0, 256)
-            idle_passes(2, x_codes[0], x_scales[0])
-            copy_wt("S", 0, 1, 0, 128)
-            copy_wt("V", 0, 0, 0, 128)
+            copy_w("S", 0, 1, 2)
+            copy_w("V", 0, 0, 1)
             quant_x(0, 256, 512)
             quant_w(0, 0, 1)
             quant_w(0, 1, 2)
-            mm(0, 0, 1, 0, 512)
-            mm(1, 0, 1, 0, 512)
-            mm(0, 1, 2, 0, 512)
-            mm(1, 1, 2, 0, 512)
-            copy_w("V", 1, 0, 80)
-            copy_w("S", 1, 80, 128)
-            quant_w(1, 0, 2)
-            idle_passes(8, w_codes[1], w_scales[1])
-            do_relu("S", 0, 0, 1, 0, 512)
-            do_relu("V", 1, 0, 1, 0, 512)
-            do_relu("S", 0, 1, 2, 0, 512)
-            do_relu("V", 1, 1, 2, 0, 512)
-            do_sq("S", 0, 0, 1, 0, 512)
+            mm(0, 0)
+            mm(1, 0)
+            mm(0, 1)
+            mm(1, 1)
+            copy_w("V", 1, 0, 1)
+            copy_w("S", 1, 1, 2, 48, 128)
+            copy_w("V", 1, 1, 2, 0, 48)
+            quant_w(1, 0, 1)
+            quant_w(1, 1, 2)
+            do_relu("S", 0, 0)
+            do_relu("V", 1, 0)
+            do_relu("S", 0, 1)
+            do_relu("V", 1, 1)
             copy_x("V", 1, 0, 256)
             copy_x("S", 1, 384, 512)
             copy_x("V", 1, 256, 384)
             quant_x(1, 0, 256)
-            idle_passes(1, x_codes[1], x_scales[1])
             quant_x(1, 256, 512)
-            mm(2, 0, 1, 0, 512)
-            mm(3, 0, 1, 0, 512)
-            mm(2, 1, 2, 0, 512)
-            mm(3, 1, 2, 0, 512)
-            do_sq("S", 0, 1, 2, 0, 512)
-            do_sq("S", 1, 0, 1, 0, 512)
-            do_sq("S", 1, 1, 2, 0, 512)
-            do_add("V", 0, 0, 1, 0, 512)
-            do_add("V", 0, 1, 2, 0, 512)
-            store(0, 0, 2, 0, 512)
-            do_add("V", 1, 0, 1, 0, 512)
-            do_add("V", 1, 1, 2, 0, 512)
-            store(1, 0, 2, 0, 512)
-            do_relu("S", 2, 0, 1, 0, 512)
-            do_relu("S", 3, 0, 1, 0, 512)
-            do_sq("S", 2, 0, 1, 0, 512)
-            do_sq("S", 3, 0, 1, 0, 512)
-            do_relu("V", 2, 1, 2, 0, 512)
-            do_relu("V", 3, 1, 2, 0, 256)
-            do_relu("S", 3, 1, 2, 256, 512)
-            do_sq("S", 2, 1, 2, 0, 512)
-            do_sq("S", 3, 1, 2, 0, 512)
-            do_add("V", 2, 0, 1, 0, 512)
-            store(2, 0, 1, 0, 512)
-            do_add("V", 3, 0, 1, 0, 512)
-            store(3, 0, 1, 0, 512)
-            do_add("V", 2, 1, 2, 0, 512)
-            store(2, 1, 2, 0, 512)
-            do_add("V", 3, 1, 2, 0, 512)
-            store(3, 1, 2, 0, 512)
+            mm(2, 0)
+            mm(2, 1)
+            mm(3, 0)
+            mm(3, 1)
+            do_sq("S", 0, 0)
+            do_sq("S", 0, 1)
+            do_sq("S", 1, 0)
+            do_sq("S", 1, 1)
+            do_add("V", 0, 0)
+            do_add("V", 0, 1)
+            store(0, 0, 2)
+            do_relu("S", 2, 0)
+            do_add("V", 1, 0)
+            do_add("V", 1, 1)
+            store(1, 0, 2)
+            do_relu("V", 3, 0)
+            do_relu("S", 2, 1)
+            do_sq("S", 2, 0)
+            do_relu("V", 3, 1, 0, 256)
+            do_sq("S", 2, 1)
+            do_sq("S", 3, 0)
+            do_relu("S", 3, 1, 256, 512)
+            do_add("V", 2, 0)
+            store(2, 0, 1)
+            do_add("V", 2, 1)
+            store(2, 1, 2)
+            do_sq("S", 3, 1, 2, 0, 256)
+            do_sq("S", 3, 1, 2, 256, 512)
+            do_add("V", 3, 0)
+            store(3, 0, 1)
+            do_add("V", 3, 1, 2, 0, 256)
+            do_add("V", 3, 1, 2, 256, 512)
+            store(3, 1, 2)

@@ -144,13 +144,14 @@ def tile_rows_glin_relu2_res_kernel(tc, x, w, r, out):
             load_x(1)
             load_r(0, 1)
             load_r(1, 2)
-            load_r(2, 4)
+            load_r(2, 3)
+            load_r(3, 4)
             copy_x("V", 0, 0, 256)
             copy_x("S", 0, 320, 512)
             copy_x("V", 0, 256, 320)
             quant_x(0, 0, 256)
-            copy_w("S", 0, 1, 2)
-            copy_w("V", 0, 0, 1)
+            copy_w("S", 0, 0, 2, 80, 128)
+            copy_w("V", 0, 0, 2, 0, 80)
             quant_x(0, 256, 512)
             quant_w(0, 0, 1)
             quant_w(0, 1, 2)
@@ -158,15 +159,14 @@ def tile_rows_glin_relu2_res_kernel(tc, x, w, r, out):
             mm(1, 0)
             mm(0, 1)
             mm(1, 1)
-            copy_w("V", 1, 0, 1)
-            copy_w("S", 1, 1, 2, 48, 128)
-            copy_w("V", 1, 1, 2, 0, 48)
-            quant_w(1, 0, 1)
-            quant_w(1, 1, 2)
+            copy_w("V", 1, 0, 2, 0, 80)
+            copy_w("S", 1, 0, 2, 80, 128)
+            quant_w(1, 0, 2)
             do_relu("S", 0, 0)
             do_relu("V", 1, 0)
             do_relu("S", 0, 1)
             do_relu("V", 1, 1)
+            do_sq("S", 0, 0)
             copy_x("V", 1, 0, 256)
             copy_x("S", 1, 384, 512)
             copy_x("V", 1, 256, 384)
@@ -176,17 +176,16 @@ def tile_rows_glin_relu2_res_kernel(tc, x, w, r, out):
             mm(2, 1)
             mm(3, 0)
             mm(3, 1)
-            do_sq("S", 0, 0)
             do_sq("S", 0, 1)
             do_sq("S", 1, 0)
             do_sq("S", 1, 1)
             do_add("V", 0, 0)
             do_add("V", 0, 1)
             store(0, 0, 2)
-            do_relu("S", 2, 0)
             do_add("V", 1, 0)
             do_add("V", 1, 1)
             store(1, 0, 2)
+            do_relu("S", 2, 0)
             do_relu("V", 3, 0)
             do_relu("S", 2, 1)
             do_sq("S", 2, 0)

@@ -30,7 +30,7 @@ def tile_rows_glin_relu2_res_kernel(tc, x, w, r, out):
         psum = ctx.enter_context(tc.psum_pool(name="psum", bufs=1))
 
         def tiles(name, count, shape, dtype):
-            return [sb.tile(shape, dtype, name="%s%d" % (name, i), align_bytes=64) for i in range(count)]
+            return [sb.tile(shape, dtype, name="%s%d" % (name, i), align_bytes=256) for i in range(count)]
 
         x_raw = tiles("x_raw", PAIRS, [P, PACK, N], F32)
         w_raw = tiles("w_raw", PAIRS, [P, PACK, M], F32)

@@ -72,13 +72,9 @@ def tile_rows_glin_relu2_res_kernel(tc, x, w, r, out):
             src = x_raw[q][:, j0:j1, n0:n1].rearrange("p j (c i) -> p c j i", i=RUN)
             copy(engine, dst, src)
 
-        def copy_w(engine, q, t0, t1, s0=0, s1=P):
-            if t1 - t0 == DEAL:
-                dst = w_bf[q][:, :, s0:s1, :].rearrange("p t (c i) j -> p c j i t", i=RUN // DEAL)
-                src = w_raw[q][:, :, DEAL * s0 : DEAL * s1].rearrange("p j (c i t) -> p c j i t", i=RUN // DEAL, t=DEAL)
-            else:
-                dst = w_bf[q][:, t0, s0:s1, :].rearrange("p (c i) j -> p c j i", i=RUN // DEAL)
-                src = w_raw[q][:, :, DEAL * s0 : DEAL * s1].rearrange("p j (c i t) -> p t c j i", i=RUN // DEAL, t=DEAL)[:, t0]
+        def copy_w(engine, q, s0, s1):
+            dst = w_bf[q][:, :, s0:s1, :].rearrange("p t (c i) j -> p c j i t", i=RUN // DEAL)
+            src = w_raw[q][:, :, DEAL * s0 : DEAL * s1].rearrange("p j (c i t) -> p c j i t", i=RUN // DEAL, t=DEAL)
             copy(engine, dst, src)
 
         def quant_x(q, n0, n1):
@@ -109,7 +105,7 @@ def tile_rows_glin_relu2_res_kernel(tc, x, w, r, out):
                 stop=True,
             )
 
-        def do_relu(engine, g, t, n0=0, n1=N):
+        def do_relu(engine, g, t, t1=None, n0=0, n1=N):
             dst = relu[g][:, t, n0:n1]
             if engine == "V":
                 nc.vector.tensor_scalar(out=dst, in0=z[g][t][:, n0:n1], scalar1=0.0, scalar2=None, op0=ALU.max)
@@ -150,8 +146,8 @@ def tile_rows_glin_relu2_res_kernel(tc, x, w, r, out):
             copy_x("S", 0, 320, 512)
             copy_x("V", 0, 256, 320)
             quant_x(0, 0, 256)
-            copy_w("S", 0, 0, 2, 80, 128)
-            copy_w("V", 0, 0, 2, 0, 80)
+            copy_w("S", 0, 80, 128)
+            copy_w("V", 0, 0, 80)
             quant_x(0, 256, 512)
             quant_w(0, 0, 1)
             quant_w(0, 1, 2)
@@ -159,17 +155,19 @@ def tile_rows_glin_relu2_res_kernel(tc, x, w, r, out):
             mm(1, 0)
             mm(0, 1)
             mm(1, 1)
-            copy_w("V", 1, 0, 2, 0, 80)
-            copy_w("S", 1, 0, 2, 80, 128)
+            copy_w("V", 1, 0, 80)
+            copy_w("S", 1, 80, 128)
             quant_w(1, 0, 2)
-            do_relu("S", 0, 0)
+            do_relu("S", 0, 0, 1, 0, 256)
+            do_relu("S", 0, 0, 1, 256, 512)
             do_relu("V", 1, 0)
             do_relu("S", 0, 1)
             do_relu("V", 1, 1)
-            do_sq("S", 0, 0)
+            do_sq("G", 0, 0, 1, 0, 256)
+            do_sq("S", 0, 0, 1, 256, 512)
             copy_x("V", 1, 0, 256)
-            copy_x("S", 1, 384, 512)
-            copy_x("V", 1, 256, 384)
+            copy_x("S", 1, 352, 512)
+            copy_x("V", 1, 256, 352)
             quant_x(1, 0, 256)
             quant_x(1, 256, 512)
             mm(2, 0)
@@ -189,10 +187,11 @@ def tile_rows_glin_relu2_res_kernel(tc, x, w, r, out):
             do_relu("V", 3, 0)
             do_relu("S", 2, 1)
             do_sq("S", 2, 0)
-            do_relu("V", 3, 1, 0, 256)
-            do_sq("S", 2, 1)
+            do_relu("V", 3, 1, 2, 0, 256)
+            do_sq("G", 2, 1, 2, 0, 192)
+            do_sq("S", 2, 1, 2, 192, 512)
             do_sq("S", 3, 0)
-            do_relu("S", 3, 1, 256, 512)
+            do_relu("S", 3, 1, 2, 256, 512)
             do_add("V", 2, 0)
             store(2, 0, 1)
             do_add("V", 2, 1)

@@ -163,17 +163,17 @@ def tile_rows_glin_relu2_res_kernel(tc, x, w, r, out):
             do_relu("V", 1, 0)
             do_relu("S", 0, 1)
             do_relu("V", 1, 1)
-            do_sq("G", 0, 0, 1, 0, 256)
-            do_sq("S", 0, 0, 1, 256, 512)
+            do_sq("G", 0, 0, 1, 0, 192)
             copy_x("V", 1, 0, 256)
             copy_x("S", 1, 352, 512)
             copy_x("V", 1, 256, 352)
             quant_x(1, 0, 256)
             quant_x(1, 256, 512)
             mm(2, 0)
-            mm(2, 1)
             mm(3, 0)
+            mm(2, 1)
             mm(3, 1)
+            do_sq("S", 0, 0, 1, 192, 512)
             do_sq("S", 0, 1)
             do_sq("S", 1, 0)
             do_sq("S", 1, 1)
@@ -183,23 +183,30 @@ def tile_rows_glin_relu2_res_kernel(tc, x, w, r, out):
             do_add("V", 1, 0)
             do_add("V", 1, 1)
             store(1, 0, 2)
-            do_relu("S", 2, 0)
+            do_relu("S", 2, 0, 1, 0, 256)
+            do_relu("S", 2, 0, 1, 256, 512)
             do_relu("V", 3, 0)
-            do_relu("S", 2, 1)
-            do_sq("S", 2, 0)
-            do_relu("V", 3, 1, 2, 0, 256)
-            do_sq("G", 2, 1, 2, 0, 192)
-            do_sq("S", 2, 1, 2, 192, 512)
-            do_sq("S", 3, 0)
-            do_relu("S", 3, 1, 2, 256, 512)
+            do_sq("S", 2, 0, 1, 0, 256)
+            do_sq("S", 2, 0, 1, 256, 512)
+            do_relu("S", 2, 1, 2, 0, 256)
+            do_relu("S", 2, 1, 2, 256, 512)
             do_add("V", 2, 0)
             store(2, 0, 1)
-            do_add("V", 2, 1)
+            do_relu("V", 3, 1, 2, 0, 256)
+            do_sq("S", 2, 1, 2, 0, 256)
+            do_sq("S", 2, 1, 2, 256, 512)
+            do_add("V", 2, 1, 2, 0, 256)
+            do_add("V", 2, 1, 2, 256, 512)
             store(2, 1, 2)
+            do_sq("S", 3, 0, 1, 0, 256)
+            do_sq("S", 3, 0, 1, 256, 512)
+            do_add("V", 3, 0, 1, 0, 256)
+            do_add("V", 3, 0, 1, 256, 512)
+            store(3, 0, 1)
+            do_relu("S", 3, 1, 2, 256, 512)
             do_sq("S", 3, 1, 2, 0, 256)
             do_sq("S", 3, 1, 2, 256, 512)
-            do_add("V", 3, 0)
-            store(3, 0, 1)
             do_add("V", 3, 1, 2, 0, 256)
+            store(3, 1, 2, 0, 256)
             do_add("V", 3, 1, 2, 256, 512)
-            store(3, 1, 2)
+            store(3, 1, 2, 256, 512)

@@ -158,12 +158,12 @@ def tile_rows_glin_relu2_res_kernel(tc, x, w, r, out):
             copy_w("V", 1, 0, 80)
             copy_w("S", 1, 80, 128)
             quant_w(1, 0, 2)
-            do_relu("S", 0, 0, 1, 0, 256)
-            do_relu("S", 0, 0, 1, 256, 512)
+            do_relu("S", 0, 0, 1, 0, 224)
+            do_relu("S", 0, 0, 1, 224, 512)
             do_relu("V", 1, 0)
             do_relu("S", 0, 1)
             do_relu("V", 1, 1)
-            do_sq("G", 0, 0, 1, 0, 192)
+            do_sq("G", 0, 0, 1, 0, 224)
             copy_x("V", 1, 0, 256)
             copy_x("S", 1, 352, 512)
             copy_x("V", 1, 256, 352)
@@ -173,7 +173,7 @@ def tile_rows_glin_relu2_res_kernel(tc, x, w, r, out):
             mm(3, 0)
             mm(2, 1)
             mm(3, 1)
-            do_sq("S", 0, 0, 1, 192, 512)
+            do_sq("S", 0, 0, 1, 224, 512)
             do_sq("S", 0, 1)
             do_sq("S", 1, 0)
             do_sq("S", 1, 1)
@@ -186,13 +186,15 @@ def tile_rows_glin_relu2_res_kernel(tc, x, w, r, out):
             do_relu("S", 2, 0, 1, 0, 256)
             do_relu("S", 2, 0, 1, 256, 512)
             do_relu("V", 3, 0)
+            do_sq("G", 2, 0, 1, 320, 512)
             do_sq("S", 2, 0, 1, 0, 256)
-            do_sq("S", 2, 0, 1, 256, 512)
             do_relu("S", 2, 1, 2, 0, 256)
+            do_sq("S", 2, 0, 1, 256, 320)
             do_relu("S", 2, 1, 2, 256, 512)
-            do_add("V", 2, 0)
+            do_relu("V", 3, 1, 2, 0, 128)
+            do_add("V", 2, 0, 1, 0, 256)
+            do_add("V", 2, 0, 1, 256, 512)
             store(2, 0, 1)
-            do_relu("V", 3, 1, 2, 0, 256)
             do_sq("S", 2, 1, 2, 0, 256)
             do_sq("S", 2, 1, 2, 256, 512)
             do_add("V", 2, 1, 2, 0, 256)
@@ -203,6 +205,7 @@ def tile_rows_glin_relu2_res_kernel(tc, x, w, r, out):
             do_add("V", 3, 0, 1, 0, 256)
             do_add("V", 3, 0, 1, 256, 512)
             store(3, 0, 1)
+            do_relu("S", 3, 1, 2, 128, 256)
             do_relu("S", 3, 1, 2, 256, 512)
             do_sq("S", 3, 1, 2, 0, 256)
             do_sq("S", 3, 1, 2, 256, 512)

@@ -68,8 +68,8 @@ def tile_rows_glin_relu2_res_kernel(tc, x, w, r, out):
                 nc.gpsimd.tensor_scalar(out=dst, in0=src, scalar1=1.0, scalar2=0.0, op0=ALU.mult, op1=ALU.add)
 
         def copy_x(engine, q, n0, n1, j0=0, j1=PACK):
-            dst = x_bf[q][:, n0:n1, j0:j1].rearrange("p (c i) j -> p c j i", i=RUN)
-            src = x_raw[q][:, j0:j1, n0:n1].rearrange("p j (c i) -> p c j i", i=RUN)
+            dst = x_bf[q][:, n0:n1, j0:j1].rearrange("p (c i) j -> p c j i", i=2)
+            src = x_raw[q][:, j0:j1, n0:n1].rearrange("p j (c i) -> p c j i", i=2)
             copy(engine, dst, src)
 
         def copy_w(engine, q, s0, s1):
@@ -161,9 +161,9 @@ def tile_rows_glin_relu2_res_kernel(tc, x, w, r, out):
             do_relu("S", 0, 0, 1, 0, 224)
             do_relu("S", 0, 0, 1, 224, 512)
             do_relu("V", 1, 0)
-            do_relu("S", 0, 1)
-            do_relu("V", 1, 1)
             do_sq("G", 0, 0, 1, 0, 224)
+            do_relu("S", 0, 1, 2, 0, 512)
+            do_relu("V", 1, 1, 2, 0, 512)
             copy_x("V", 1, 0, 256)
             copy_x("S", 1, 352, 512)
             copy_x("V", 1, 256, 352)
@@ -192,8 +192,8 @@ def tile_rows_glin_relu2_res_kernel(tc, x, w, r, out):
             do_sq("S", 2, 0, 1, 256, 320)
             do_relu("S", 2, 1, 2, 256, 512)
             do_relu("V", 3, 1, 2, 0, 128)
-            do_add("V", 2, 0, 1, 0, 256)
-            do_add("V", 2, 0, 1, 256, 512)
+            do_add("V", 2, 0, 1, 0, 320)
+            do_add("V", 2, 0, 1, 320, 512)
             store(2, 0, 1)
             do_sq("S", 2, 1, 2, 0, 256)
             do_sq("S", 2, 1, 2, 256, 512)

@@ -46,9 +46,9 @@ def tile_rows_glin_relu2_res_kernel(tc, x, w, r, out):
         result = tiles("result", G, [P, DEAL, N], F32)
         z = [[psum.tile([P, N], F32, name="z%d%d" % (g, t)) for t in range(DEAL)] for g in range(G)]
 
-        def load_x(q, j0=0, j1=PACK):
+        def load_x(q, j0=0, j1=PACK, queue=nc.sync):
             src = x[SIDE * q : SIDE * (q + 1)].rearrange("c (p j) n -> (c p) j n", j=PACK)
-            nc.sync.dma_start(out=x_raw[q][:, j0:j1], in_=src[:, j0:j1])
+            queue.dma_start(out=x_raw[q][:, j0:j1], in_=src[:, j0:j1])
 
         def load_w(q):
             src = w[SIDE * q : SIDE * (q + 1)].rearrange("c (p j) m -> (c p) j m", j=PACK)
@@ -134,7 +134,8 @@ def tile_rows_glin_relu2_res_kernel(tc, x, w, r, out):
             nc.sync.dma_start(out=dst[:, t0:t1, n0:n1], in_=result[g][:, t0:t1, n0:n1])
 
         with tc.manual_schedule():
-            load_x(0)
+            load_x(0, 0, 2)
+            load_x(0, 2, 4, nc.scalar)
             load_w(0)
             load_w(1)
             load_x(1)

@@ -44,6 +44,7 @@ def tile_rows_glin_relu2_res_kernel(tc, x, w, r, out):
         relu = tiles("relu", G, [P, DEAL, N], F32)
         sq = tiles("sq", G, [P, DEAL, N], F32)
         result = tiles("result", G, [P, DEAL, N], F32)
+        warm = tiles("warm", 2, [P, 8], F32)
         z = [[psum.tile([P, N], F32, name="z%d%d" % (g, t)) for t in range(DEAL)] for g in range(G)]
 
         def load_x(q, j0=0, j1=PACK, queue=nc.sync):
@@ -136,6 +137,8 @@ def tile_rows_glin_relu2_res_kernel(tc, x, w, r, out):
         with tc.manual_schedule():
             load_x(0, 0, 2)
             load_x(0, 2, 4, nc.scalar)
+            nc.vector.memset(warm[0][:], 0.0)
+            nc.scalar.activation(out=warm[1][:], in_=warm[0][:], func=ACT.Relu)
             load_w(0)
             load_w(1)
             load_x(1)

@@ -195,7 +195,7 @@ def tile_rows_glin_relu2_res_kernel(tc, x, w, r, out):
             do_relu("S", 2, 1, 2, 0, 256)
             do_sq("S", 2, 0, 1, 256, 320)
             do_relu("S", 2, 1, 2, 256, 512)
-            do_relu("V", 3, 1, 2, 0, 128)
+            do_relu("V", 3, 1, 2, 0, 96)
             do_add("V", 2, 0, 1, 0, 320)
             do_add("V", 2, 0, 1, 320, 512)
             store(2, 0, 1)
@@ -204,16 +204,15 @@ def tile_rows_glin_relu2_res_kernel(tc, x, w, r, out):
             do_add("V", 2, 1, 2, 0, 256)
             do_add("V", 2, 1, 2, 256, 512)
             store(2, 1, 2)
-            do_sq("S", 3, 0, 1, 0, 256)
-            do_sq("S", 3, 0, 1, 256, 512)
-            do_add("V", 3, 0, 1, 0, 256)
-            do_add("V", 3, 0, 1, 256, 512)
+            do_sq("V", 3, 0, 1, 336, 512)
+            do_sq("S", 3, 0, 1, 0, 336)
+            do_add("V", 3, 0, 1, 0, 336)
+            do_add("V", 3, 0, 1, 336, 512)
             store(3, 0, 1)
-            do_relu("S", 3, 1, 2, 128, 256)
+            do_relu("S", 3, 1, 2, 96, 256)
             do_relu("S", 3, 1, 2, 256, 512)
             do_sq("S", 3, 1, 2, 0, 256)
             do_sq("S", 3, 1, 2, 256, 512)
             do_add("V", 3, 1, 2, 0, 256)
-            store(3, 1, 2, 0, 256)
             do_add("V", 3, 1, 2, 256, 512)
-            store(3, 1, 2, 256, 512)
+            store(3, 1, 2)

@@ -168,6 +168,7 @@ def tile_rows_glin_relu2_res_kernel(tc, x, w, r, out):
             do_sq("G", 0, 0, 1, 0, 224)
             do_relu("S", 0, 1, 2, 0, 512)
             do_relu("V", 1, 1, 2, 0, 512)
+            do_sq("S", 0, 0, 1, 224, 320)
             copy_x("V", 1, 0, 256)
             copy_x("S", 1, 352, 512)
             copy_x("V", 1, 256, 352)
@@ -177,7 +178,7 @@ def tile_rows_glin_relu2_res_kernel(tc, x, w, r, out):
             mm(3, 0)
             mm(2, 1)
             mm(3, 1)
-            do_sq("S", 0, 0, 1, 224, 512)
+            do_sq("S", 0, 0, 1, 320, 512)
             do_sq("S", 0, 1)
             do_sq("S", 1, 0)
             do_sq("S", 1, 1)

from contextlib import ExitStack

import concourse.mybir as mybir

G, D, M, N = 4, 256, 256, 512
FLOPS = 2 * G * D * M * N

F32 = mybir.dt.float32
BF16 = mybir.dt.bfloat16
U32 = mybir.dt.uint32
U8 = mybir.dt.uint8
FP8X4 = mybir.dt.float8_e4m3fn_x4
ACT = mybir.ActivationFunctionType
ALU = mybir.AluOpType

P = 128
PACK = 4
ROWS = D // PACK
SIDE = P // ROWS
PAIRS = G // SIDE
DEAL = M // P
RUN = 4
HALF = N // 2


def tile_rows_glin_relu2_res_kernel(tc, x, w, r, out):
    nc = tc.nc
    with ExitStack() as ctx:
        sb = ctx.enter_context(tc.tile_pool(name="sb", bufs=1))
        psum = ctx.enter_context(tc.psum_pool(name="psum", bufs=1))

        def tiles(name, count, shape, dtype):
            return [sb.tile(shape, dtype, name="%s%d" % (name, i), align_bytes=256) for i in range(count)]

        x_raw = tiles("x_raw", PAIRS, [P, PACK, N], F32)
        w_raw = tiles("w_raw", PAIRS, [P, PACK, M], F32)
        x_bf = tiles("x_bf", PAIRS, [P, N, PACK], BF16)
        w_bf = tiles("w_bf", PAIRS, [P, DEAL, P, PACK], BF16)
        x_codes = tiles("x_codes", PAIRS, [P, N], U32)
        x_scales = tiles("x_scales", PAIRS, [P, N], U8)
        w_codes = tiles("w_codes", PAIRS, [P, M], U32)
        w_scales = tiles("w_scales", PAIRS, [P, M], U8)
        res = tiles("res", PAIRS, [P, SIDE, DEAL, N], F32)
        relu = tiles("relu", G, [P, DEAL, N], F32)
        sq = tiles("sq", G, [P, DEAL, N], F32)
        result = tiles("result", G, [P, DEAL, N], F32)
        warm = tiles("warm", 2, [P, 8], F32)
        z = [[psum.tile([P, N], F32, name="z%d%d" % (g, t)) for t in range(DEAL)] for g in range(G)]

        def load_x(q, j0=0, j1=PACK, queue=nc.sync):
            src = x[SIDE * q : SIDE * (q + 1)].rearrange("c (p j) n -> (c p) j n", j=PACK)
            queue.dma_start(out=x_raw[q][:, j0:j1], in_=src[:, j0:j1])

        def load_w(q):
            src = w[SIDE * q : SIDE * (q + 1)].rearrange("c (p j) m -> (c p) j m", j=PACK)
            nc.sync.dma_start(out=w_raw[q][:], in_=src)

        def load_r(g0, g1):
            src = r[g0:g1].rearrange("c (p t) n -> p c t n", t=DEAL)
            q, c = divmod(g0, SIDE)
            nc.sync.dma_start(out=res[q][:, c : c + g1 - g0], in_=src)

        def copy(engine, dst, src):
            if engine == "V":
                nc.vector.tensor_copy(out=dst, in_=src)
            elif engine == "S":
                nc.scalar.copy(out=dst, in_=src)
            else:
                nc.gpsimd.tensor_scalar(out=dst, in0=src, scalar1=1.0, scalar2=0.0, op0=ALU.mult, op1=ALU.add)

        def copy_x(engine, q, n0, n1, j0=0, j1=PACK):
            dst = x_bf[q][:, n0:n1, j0:j1].rearrange("p (c i) j -> p c j i", i=2)
            src = x_raw[q][:, j0:j1, n0:n1].rearrange("p j (c i) -> p c j i", i=2)
            copy(engine, dst, src)

        def copy_w(engine, q, s0, s1):
            dst = w_bf[q][:, :, s0:s1, :].rearrange("p t (c i) j -> p c j i t", i=RUN // DEAL)
            src = w_raw[q][:, :, DEAL * s0 : DEAL * s1].rearrange("p j (c i t) -> p c j i t", i=RUN // DEAL, t=DEAL)
            copy(engine, dst, src)

        def quant_x(q, n0, n1):
            nc.vector.quantize_mx(
                out=x_codes[q][:, n0:n1].bitcast(FP8X4),
                scales=x_scales[q][:, n0:n1],
                in_=x_bf[q][:, n0:n1, :].rearrange("p n j -> p (n j)"),
            )

        def quant_w(q, t0, t1):
            nc.vector.quantize_mx(
                out=w_codes[q][:, P * t0 : P * t1].bitcast(FP8X4),
                scales=w_scales[q][:, P * t0 : P * t1],
                in_=w_bf[q][:, t0:t1].rearrange("p t s j -> p (t s j)"),
            )

        def mm(g, t):
            q, c = divmod(g, SIDE)
            rows = slice(ROWS * c, ROWS * (c + 1))
            cols = slice(P * t, P * (t + 1))
            nc.tensor.matmul_mx(
                out=z[g][t][:],
                lhsT=w_codes[q][rows, cols].bitcast(FP8X4),
                lhsT_scale=w_scales[q][rows, cols],
                rhs=x_codes[q][rows, :].bitcast(FP8X4),
                rhs_scale=x_scales[q][rows, :],
                start=True,
                stop=True,
            )

        def do_relu(engine, g, t, t1=None, n0=0, n1=N):
            dst = relu[g][:, t, n0:n1]
            if engine == "V":
                nc.vector.tensor_scalar(out=dst, in0=z[g][t][:, n0:n1], scalar1=0.0, scalar2=None, op0=ALU.max)
            else:
                nc.scalar.activation(out=dst, in_=z[g][t][:, n0:n1], func=ACT.Relu)

        def do_sq(engine, g, t0, t1=None, n0=0, n1=N):
            t1 = t0 + 1 if t1 is None else t1
            dst = sq[g][:, t0:t1, n0:n1]
            src = relu[g][:, t0:t1, n0:n1]
            if engine == "V":
                nc.vector.tensor_tensor(out=dst[:, 0], in0=z[g][t0][:, n0:n1], in1=src[:, 0], op=ALU.mult)
            elif engine == "S":
                nc.scalar.activation(out=dst, in_=src, func=ACT.Square)
            else:
                nc.gpsimd.tensor_tensor(out=dst, in0=src, in1=src, op=ALU.mult)

        def do_add(engine, g, t0, t1=None, n0=0, n1=N):
            t1 = t0 + 1 if t1 is None else t1
            q, c = divmod(g, SIDE)
            eng = nc.vector if engine == "V" else nc.gpsimd
            eng.tensor_tensor(out=result[g][:, t0:t1, n0:n1], in0=sq[g][:, t0:t1, n0:n1], in1=res[q][:, c, t0:t1, n0:n1], op=ALU.add)

        def store(g, t0, t1, n0=0, n1=N):
            dst = out[g].rearrange("(p t) n -> p t n", t=DEAL)
            nc.sync.dma_start(out=dst[:, t0:t1, n0:n1], in_=result[g][:, t0:t1, n0:n1])

        with tc.manual_schedule():
            load_x(0, 0, 2)
            load_x(0, 2, 4, nc.scalar)
            nc.vector.memset(warm[0][:], 0.0)
            nc.scalar.activation(out=warm[1][:], in_=warm[0][:], func=ACT.Relu)
            load_w(0)
            load_w(1)
            load_x(1)
            load_r(0, 1)
            load_r(1, 2)
            load_r(2, 3)
            load_r(3, 4)
            copy_x("V", 0, 0, 256)
            copy_x("S", 0, 320, 512)
            copy_x("V", 0, 256, 320)
            quant_x(0, 0, 256)
            copy_w("S", 0, 80, 128)
            copy_w("V", 0, 0, 80)
            quant_x(0, 256, 512)
            quant_w(0, 0, 1)
            quant_w(0, 1, 2)
            mm(0, 0)
            mm(1, 0)
            mm(0, 1)
            mm(1, 1)
            copy_w("V", 1, 0, 80)
            copy_w("S", 1, 80, 128)
            quant_w(1, 0, 2)
            do_relu("S", 0, 0, 1, 0, 224)
            do_relu("S", 0, 0, 1, 224, 512)
            do_relu("V", 1, 0)
            do_sq("G", 0, 0, 1, 0, 224)
            do_relu("S", 0, 1, 2, 0, 512)
            do_relu("V", 1, 1, 2, 0, 512)
            do_sq("S", 0, 0, 1, 224, 320)
            copy_x("V", 1, 0, 256)
            copy_x("S", 1, 352, 512)
            copy_x("V", 1, 256, 352)
            quant_x(1, 0, 256)
            quant_x(1, 256, 512)
            mm(2, 0)
            mm(3, 0)
            mm(2, 1)
            mm(3, 1)
            do_sq("S", 0, 0, 1, 320, 512)
            do_sq("S", 0, 1)
            do_sq("S", 1, 0)
            do_sq("S", 1, 1)
            do_add("V", 0, 0)
            do_add("V", 0, 1)
            store(0, 0, 2)
            do_add("V", 1, 0)
            do_add("V", 1, 1)
            store(1, 0, 2)
            do_relu("S", 2, 0, 1, 0, 256)
            do_relu("S", 2, 0, 1, 256, 512)
            do_relu("V", 3, 0)
            do_sq("G", 2, 0, 1, 320, 512)
            do_sq("S", 2, 0, 1, 0, 256)
            do_relu("S", 2, 1, 2, 0, 256)
            do_sq("S", 2, 0, 1, 256, 320)
            do_relu("S", 2, 1, 2, 256, 512)
            do_relu("V", 3, 1, 2, 0, 96)
            do_add("V", 2, 0, 1, 0, 320)
            do_add("V", 2, 0, 1, 320, 512)
            store(2, 0, 1)
            do_sq("S", 2, 1, 2, 0, 256)
            do_sq("S", 2, 1, 2, 256, 512)
            do_add("V", 2, 1, 2, 0, 256)
            do_add("V", 2, 1, 2, 256, 512)
            store(2, 1, 2)
            do_sq("V", 3, 0, 1, 336, 512)
            do_sq("S", 3, 0, 1, 0, 336)
            do_add("V", 3, 0, 1, 0, 336)
            do_add("V", 3, 0, 1, 336, 512)
            store(3, 0, 1)
            do_relu("S", 3, 1, 2, 96, 256)
            do_relu("S", 3, 1, 2, 256, 512)
            do_sq("S", 3, 1, 2, 0, 256)
            do_sq("S", 3, 1, 2, 256, 512)
            do_add("V", 3, 1, 2, 0, 256)
            do_add("V", 3, 1, 2, 256, 512)
            store(3, 1, 2)
